import numpy as np
import ml_dtypes

BF16 = ml_dtypes.bfloat16


def bf(x):
    return np.asarray(x, np.float32).astype(BF16)


def f32(x):
    return np.asarray(x, np.float32)


def f64(x):
    return np.asarray(x).astype(np.float64)


def striped(idx):
    return np.tile(idx.reshape(-1, 16).T, (8, 1))


S, K, M, N = 2048, 128, 512, 2048


def setup_inputs():
    return {"table": bf(np.random.standard_normal((K, S))), "w": bf(np.random.standard_normal((K, M)) / np.sqrt(K)), "r": f32(np.random.standard_normal((M, N))), "offs": striped(np.random.permutation(S))}


def reference(table, w, r, offs):
    idx = offs[:16].T.reshape(-1)
    x = f64(table)[:, idx]
    y = f64(w).T @ x
    return y + f64(r)

@@ -1,0 +1,45 @@
+import concourse.mybir as mybir
+
+BF16, F32, U16 = mybir.dt.bfloat16, mybir.dt.float32, mybir.dt.uint16
+ADD = mybir.AluOpType.add
+
+P = 128
+S = 2048
+M = 512
+N = 2048
+PIECE = 512
+PIECE_COLS = PIECE // 16
+BLOCKS = M // P
+PIECES = N // PIECE
+PSUM_BANKS = 8
+
+FLOPS = 2 * P * M * N
+
+
+def tile_gather_matmul_kernel(tc, table, w, r, offs, out):
+    nc = tc.nc
+    with (
+        tc.tile_pool(name="held", bufs=1) as held,
+        tc.psum_pool(name="psum", bufs=PSUM_BANKS) as psum,
+    ):
+        offsets = held.tile([P, N // 16], U16, name="offsets")
+        nc.sync.dma_start(offsets[:], offs)
+        weights = held.tile([P, M], BF16, name="weights")
+        nc.scalar.dma_start(weights[:], w)
+        tokens = held.tile([P, S], BF16, name="tokens")
+        nc.sync.dma_start(tokens[:], table)
+
+        sums = []
+        for b in range(BLOCKS):
+            block = held.tile([P, N], F32, name="sums%d" % b)
+            nc.sync.dma_start(block[:], r[b * P : (b + 1) * P, :])
+            sums.append(block)
+
+        for b in range(BLOCKS):
+            for q in range(PIECES):
+                picked = tokens[:].indirect(offsets[:, q * PIECE_COLS : (q + 1) * PIECE_COLS])
+                bank = psum.tile([P, PIECE], F32, name="bank")
+                nc.tensor.matmul(bank[:], weights[:, b * P : (b + 1) * P], picked, start=True, stop=True)
+                columns = sums[b][:, q * PIECE : (q + 1) * PIECE]
+                nc.vector.tensor_tensor(columns, bank[:], columns, ADD)
+            nc.scalar.dma_start(out[b * P : (b + 1) * P, :], sums[b][:])

@@ -42,4 +42,4 @@ def tile_gather_matmul_kernel(tc, table, w, r, offs, out):
                 nc.tensor.matmul(bank[:], weights[:, b * P : (b + 1) * P], picked, start=True, stop=True)
                 columns = sums[b][:, q * PIECE : (q + 1) * PIECE]
                 nc.vector.tensor_tensor(columns, bank[:], columns, ADD)
-            nc.scalar.dma_start(out[b * P : (b + 1) * P, :], sums[b][:])
+            nc.sync.dma_start(out[b * P : (b + 1) * P, :], sums[b][:])

@@ -42,4 +42,7 @@ def tile_gather_matmul_kernel(tc, table, w, r, offs, out):
                 nc.tensor.matmul(bank[:], weights[:, b * P : (b + 1) * P], picked, start=True, stop=True)
                 columns = sums[b][:, q * PIECE : (q + 1) * PIECE]
                 nc.vector.tensor_tensor(columns, bank[:], columns, ADD)
-            nc.sync.dma_start(out[b * P : (b + 1) * P, :], sums[b][:])
+                if b == BLOCKS - 1:
+                    nc.scalar.dma_start(out[b * P : (b + 1) * P, q * PIECE : (q + 1) * PIECE], columns)
+            if b < BLOCKS - 1:
+                nc.scalar.dma_start(out[b * P : (b + 1) * P, :], sums[b][:])

@@ -25,7 +25,7 @@ def tile_gather_matmul_kernel(tc, table, w, r, offs, out):
         offsets = held.tile([P, N // 16], U16, name="offsets")
         nc.sync.dma_start(offsets[:], offs)
         weights = held.tile([P, M], BF16, name="weights")
-        nc.scalar.dma_start(weights[:], w)
+        nc.sync.dma_start(weights[:], w)
         tokens = held.tile([P, S], BF16, name="tokens")
         nc.sync.dma_start(tokens[:], table)
 
@@ -43,6 +43,6 @@ def tile_gather_matmul_kernel(tc, table, w, r, offs, out):
                 columns = sums[b][:, q * PIECE : (q + 1) * PIECE]
                 nc.vector.tensor_tensor(columns, bank[:], columns, ADD)
                 if b == BLOCKS - 1:
-                    nc.scalar.dma_start(out[b * P : (b + 1) * P, q * PIECE : (q + 1) * PIECE], columns)
+                    nc.sync.dma_start(out[b * P : (b + 1) * P, q * PIECE : (q + 1) * PIECE], columns)
             if b < BLOCKS - 1:
-                nc.scalar.dma_start(out[b * P : (b + 1) * P, :], sums[b][:])
+                nc.sync.dma_start(out[b * P : (b + 1) * P, :], sums[b][:])

@@ -22,12 +22,12 @@ def tile_gather_matmul_kernel(tc, table, w, r, offs, out):
         tc.tile_pool(name="held", bufs=1) as held,
         tc.psum_pool(name="psum", bufs=PSUM_BANKS) as psum,
     ):
+        tokens = held.tile([P, S], BF16, name="tokens")
+        nc.sync.dma_start(tokens[:], table)
         offsets = held.tile([P, N // 16], U16, name="offsets")
         nc.sync.dma_start(offsets[:], offs)
         weights = held.tile([P, M], BF16, name="weights")
         nc.sync.dma_start(weights[:], w)
-        tokens = held.tile([P, S], BF16, name="tokens")
-        nc.sync.dma_start(tokens[:], table)
 
         sums = []
         for b in range(BLOCKS):

@@ -18,6 +18,8 @@ FLOPS = 2 * P * M * N
 
 def tile_gather_matmul_kernel(tc, table, w, r, offs, out):
     nc = tc.nc
+    r_rows = r.rearrange("(p a) n -> p (a n)", a=BLOCKS)
+    out_rows = out.rearrange("(p a) n -> p (a n)", a=BLOCKS)
     with (
         tc.tile_pool(name="held", bufs=1) as held,
         tc.psum_pool(name="psum", bufs=PSUM_BANKS) as psum,
@@ -29,20 +31,26 @@ def tile_gather_matmul_kernel(tc, table, w, r, offs, out):
         weights = held.tile([P, M], BF16, name="weights")
         nc.sync.dma_start(weights[:], w)
 
-        sums = []
-        for b in range(BLOCKS):
-            block = held.tile([P, N], F32, name="sums%d" % b)
-            nc.sync.dma_start(block[:], r[b * P : (b + 1) * P, :])
-            sums.append(block)
+        sums = held.tile([P, BLOCKS * N], F32, name="sums")
+        half = BLOCKS * N // 2
+        for h in range(2):
+            nc.sync.dma_start(sums[:, h * half : (h + 1) * half], r_rows[:, h * half : (h + 1) * half])
 
-        for b in range(BLOCKS):
+        grouped = held.tile([P, M], BF16, name="grouped")
+        nc.vector.tensor_copy(
+            grouped[:].rearrange("k (a p) -> k a p", a=BLOCKS),
+            weights[:].rearrange("k (p a) -> k a p", a=BLOCKS),
+        )
+
+        for a in range(BLOCKS):
+            together = PIECES if a < BLOCKS // 2 else PIECES // 2
             for q in range(PIECES):
                 picked = tokens[:].indirect(offsets[:, q * PIECE_COLS : (q + 1) * PIECE_COLS])
                 bank = psum.tile([P, PIECE], F32, name="bank")
-                nc.tensor.matmul(bank[:], weights[:, b * P : (b + 1) * P], picked, start=True, stop=True)
-                columns = sums[b][:, q * PIECE : (q + 1) * PIECE]
+                nc.tensor.matmul(bank[:], grouped[:, a * P : (a + 1) * P], picked, start=True, stop=True)
+                end = a * N + (q + 1) * PIECE
+                columns = sums[:, end - PIECE : end]
                 nc.vector.tensor_tensor(columns, bank[:], columns, ADD)
-                if b == BLOCKS - 1:
-                    nc.sync.dma_start(out[b * P : (b + 1) * P, q * PIECE : (q + 1) * PIECE], columns)
-            if b < BLOCKS - 1:
-                nc.sync.dma_start(out[b * P : (b + 1) * P, :], sums[b][:])
+                if (q + 1) % together == 0:
+                    summed = slice(end - together * PIECE, end)
+                    nc.sync.dma_start(out_rows[:, summed], sums[:, summed])

@@ -43,7 +43,8 @@ def tile_gather_matmul_kernel(tc, table, w, r, offs, out):
         )
 
         for a in range(BLOCKS):
-            together = PIECES if a < BLOCKS // 2 else PIECES // 2
+            stores_end_at = [PIECES] if a < BLOCKS - 1 else [PIECES // 2, PIECES - 1, PIECES]
+            stored = 0
             for q in range(PIECES):
                 picked = tokens[:].indirect(offsets[:, q * PIECE_COLS : (q + 1) * PIECE_COLS])
                 bank = psum.tile([P, PIECE], F32, name="bank")
@@ -51,6 +52,7 @@ def tile_gather_matmul_kernel(tc, table, w, r, offs, out):
                 end = a * N + (q + 1) * PIECE
                 columns = sums[:, end - PIECE : end]
                 nc.vector.tensor_tensor(columns, bank[:], columns, ADD)
-                if (q + 1) % together == 0:
-                    summed = slice(end - together * PIECE, end)
+                if q + 1 in stores_end_at:
+                    summed = slice(a * N + stored * PIECE, end)
                     nc.sync.dma_start(out_rows[:, summed], sums[:, summed])
+                    stored = q + 1

@@ -43,7 +43,7 @@ def tile_gather_matmul_kernel(tc, table, w, r, offs, out):
         )
 
         for a in range(BLOCKS):
-            stores_end_at = [PIECES] if a < BLOCKS - 1 else [PIECES // 2, PIECES - 1, PIECES]
+            stores_end_at = [PIECES] if a < BLOCKS - 1 else [1, 2, 3, 4]
             stored = 0
             for q in range(PIECES):
                 picked = tokens[:].indirect(offsets[:, q * PIECE_COLS : (q + 1) * PIECE_COLS])

import concourse.mybir as mybir

BF16, F32, U16 = mybir.dt.bfloat16, mybir.dt.float32, mybir.dt.uint16
ADD = mybir.AluOpType.add

P = 128
S = 2048
M = 512
N = 2048
PIECE = 512
PIECE_COLS = PIECE // 16
BLOCKS = M // P
PIECES = N // PIECE
PSUM_BANKS = 8

FLOPS = 2 * P * M * N


def tile_gather_matmul_kernel(tc, table, w, r, offs, out):
    nc = tc.nc
    r_rows = r.rearrange("(p a) n -> p (a n)", a=BLOCKS)
    out_rows = out.rearrange("(p a) n -> p (a n)", a=BLOCKS)
    with (
        tc.tile_pool(name="held", bufs=1) as held,
        tc.psum_pool(name="psum", bufs=PSUM_BANKS) as psum,
    ):
        tokens = held.tile([P, S], BF16, name="tokens")
        nc.sync.dma_start(tokens[:], table)
        offsets = held.tile([P, N // 16], U16, name="offsets")
        nc.sync.dma_start(offsets[:], offs)
        weights = held.tile([P, M], BF16, name="weights")
        nc.sync.dma_start(weights[:], w)

        sums = held.tile([P, BLOCKS * N], F32, name="sums")
        half = BLOCKS * N // 2
        for h in range(2):
            nc.sync.dma_start(sums[:, h * half : (h + 1) * half], r_rows[:, h * half : (h + 1) * half])

        grouped = held.tile([P, M], BF16, name="grouped")
        nc.vector.tensor_copy(
            grouped[:].rearrange("k (a p) -> k a p", a=BLOCKS),
            weights[:].rearrange("k (p a) -> k a p", a=BLOCKS),
        )

        for a in range(BLOCKS):
            stores_end_at = [PIECES] if a < BLOCKS - 1 else [1, 2, 3, 4]
            stored = 0
            for q in range(PIECES):
                picked = tokens[:].indirect(offsets[:, q * PIECE_COLS : (q + 1) * PIECE_COLS])
                bank = psum.tile([P, PIECE], F32, name="bank")
                nc.tensor.matmul(bank[:], grouped[:, a * P : (a + 1) * P], picked, start=True, stop=True)
                end = a * N + (q + 1) * PIECE
                columns = sums[:, end - PIECE : end]
                nc.vector.tensor_tensor(columns, bank[:], columns, ADD)
                if q + 1 in stores_end_at:
                    summed = slice(a * N + stored * PIECE, end)
                    nc.sync.dma_start(out_rows[:, summed], sums[:, summed])
                    stored = q + 1
